import numpy as np
import ml_dtypes


def mxq(x, axis, fmt="e4m3"):
    dtype, down = {"e4m3": (ml_dtypes.float8_e4m3fn, 7), "e5m2": (ml_dtypes.float8_e5m2, 14)}[fmt]
    v = np.moveaxis(np.asarray(x, np.float32).astype(ml_dtypes.bfloat16).astype(np.float64), axis, -1)
    blocks = v.reshape(v.shape[:-1] + (-1, 32))
    amax = np.abs(blocks).max(-1, keepdims=True)
    byte = np.maximum(np.where(amax > 0, np.frexp(amax)[1] - 1 + 127, 0) - down, 1)
    scale = np.exp2(byte - 127.0)
    codes = (blocks / scale).astype(np.float32).astype(dtype).astype(np.float64)
    return np.moveaxis((codes * scale).reshape(v.shape), -1, axis)


WIDE = False


def mx_kscale(k):
    if not WIDE:
        return np.ones(k)
    levels = np.array([30, -30])
    if k % 512:
        return np.exp2(np.random.permutation(np.resize(levels, k // 32))).repeat(32)
    a = np.empty((k // 512, 16))
    for p in range(k // 512):
        a[p, :8] = np.random.permutation(np.resize(levels, 8))
        for g in range(8):
            far = levels[np.abs(levels - a[p, g]) >= 10]
            a[p, g + 8] = far[np.random.randint(len(far))]
    return np.exp2(a.ravel()).repeat(32)


def f64(x):
    return np.asarray(x).astype(np.float64)


def striped(idx):
    return np.tile(np.asarray(idx).reshape(-1, 16).T, (8, 1)).astype(np.uint16)


def unstriped(offs):
    return offs[:16].T.reshape(-1).astype(np.int64)


E2M1 = np.array([0.0, 0.5, 1.0, 1.5, 2.0, 3.0, 4.0, 6.0, -0.0, -0.5, -1.0, -1.5, -2.0, -3.0, -4.0, -6.0])


def pack_weight(w, fmt):
    k, n = w.shape
    w = f64(np.asarray(w, np.float32).astype(ml_dtypes.bfloat16)).reshape(k // 32, 32, n)
    amax = np.abs(w).max(1)
    if fmt in ("e4m3", "e5m2"):
        byte = np.frexp(amax)[1] - 1 + 127 - (7 if fmt == "e4m3" else 14)
    else:
        mant, ex = np.frexp(amax / 6.0)
        byte = np.where(mant > 0.5, ex, ex - 1) + 127
    byte = np.clip(np.where(amax > 0, byte, 1), 1, 254)
    scaled = (w * np.exp2(127.0 - byte)[:, None, :]).reshape(k, n).astype(np.float32)
    by_word = np.ascontiguousarray(scaled.reshape(k // 512, 128, 4, n).transpose(0, 1, 3, 2))
    if fmt in ("e4m3", "e5m2"):
        words = by_word.astype(ml_dtypes.float8_e4m3fn if fmt == "e4m3" else ml_dtypes.float8_e5m2).view(np.uint8)
    else:
        c = by_word.astype(ml_dtypes.float4_e2m1fn).view(np.uint8) & 0xF
        words = (c[..., 0::2] | (c[..., 1::2] << 4)).reshape(k // 512, 128, 2 * n)
    return np.ascontiguousarray(words), np.ascontiguousarray(byte.astype(np.uint8).reshape(k // 512, 16, n))


def unpack_weight(words, scales, fmt):
    g, _, n = scales.shape
    words = np.ascontiguousarray(words).reshape(g, 128, n, -1)
    if fmt in ("e4m3", "e5m2"):
        vals = words.view(ml_dtypes.float8_e4m3fn if fmt == "e4m3" else ml_dtypes.float8_e5m2).astype(np.float64)
    else:
        nib = np.empty((g, 128, n, 4), np.uint8)
        nib[..., 0::2] = words & 0xF
        nib[..., 1::2] = words >> 4
        vals = E2M1[nib]
    vals = vals * np.repeat(np.exp2(scales.astype(np.float64) - 127.0), 8, axis=1)[..., None]
    return vals.transpose(0, 1, 3, 2).reshape(g * 512, n)


K, F, T, Z, J, R, C, N, E = 512, 512, 1024, 1024, 256, 512, 512, 256, 1024


def setup_inputs():
    n = np.random.standard_normal
    idx = np.random.permutation(T)[:J]
    idx2 = np.random.permutation(Z)[:J]
    idx3 = np.random.permutation(C)[:J]
    idx4 = np.random.permutation(C)[:J]
    idx5 = np.random.permutation(T)[:J]
    idx6 = np.random.permutation(E)[:J]
    fk = mx_kscale(K)
    fr = mx_kscale(R)
    ff = mx_kscale(F)
    xtp = pack_weight(n((K, T)) / fk[:, None], "e2m1")
    wp = pack_weight(n((K, R)) * 1 / np.sqrt(K) * fk[:, None] * fr, "e5m2")
    xop = pack_weight(n((F, Z)) / ff[:, None], "e5m2")
    w0p = pack_weight(n((F, R)) * 1 / np.sqrt(F) * ff[:, None] * fr, "e4m3")
    wbp = pack_weight(n((R, N)) * 1 / np.sqrt(R) / fr[:, None], "e4m3")
    wsp = pack_weight(n((K, N)) * 1 / np.sqrt(K) * fk[:, None], "e4m3")
    return {
        "xt_words": xtp[0],
        "xt_scales": xtp[1],
        "w_words": wp[0],
        "w_scales": wp[1],
        "xo_words": xop[0],
        "xo_scales": xop[1],
        "w0_words": w0p[0],
        "w0_scales": w0p[1],
        "wb_words": wbp[0],
        "wb_scales": wbp[1],
        "ws_words": wsp[0],
        "ws_scales": wsp[1],
        "tz": (n((N, E))).astype(np.float32),
        "offs": striped(idx),
        "offs2": striped(idx2),
        "offs3": striped(idx3),
        "offs4": striped(idx4),
        "offs5": striped(idx5),
        "offs6": striped(idx6),
    }


def reference(xt_words, xt_scales, w_words, w_scales, xo_words, xo_scales, w0_words, w0_scales, wb_words, wb_scales, ws_words, ws_scales, tz, offs, offs2, offs3, offs4, offs5, offs6):
    idx = unstriped(offs)
    idx2 = unstriped(offs2)
    idx3 = unstriped(offs3)
    idx4 = unstriped(offs4)
    idx5 = unstriped(offs5)
    idx6 = unstriped(offs6)
    xtu = unpack_weight(xt_words, xt_scales, "e2m1")
    wu = unpack_weight(w_words, w_scales, "e5m2")
    xou = unpack_weight(xo_words, xo_scales, "e5m2")
    w0u = unpack_weight(w0_words, w0_scales, "e4m3")
    wbu = unpack_weight(wb_words, wb_scales, "e4m3")
    wsu = unpack_weight(ws_words, ws_scales, "e4m3")
    xtidxg = xtu[:, idx]
    xoidx2g = xou[:, idx2]
    a = wu.T @ xtidxg + w0u.T @ xoidx2g
    pw = np.zeros((R, C))
    pw[:, idx3] = a
    hid = np.abs(pw[:, idx4] - a)
    hidq = mxq(hid, 0, "e5m2")
    xtidx5g = xtu[:, idx5]
    p = wbu.T @ hidq + wsu.T @ xtidx5g
    y = p + f64(tz)[:, idx6]
    return y

@@ -1,0 +1,188 @@
+from contextlib import ExitStack
+
+import concourse.mybir as mybir
+
+K, T, Z, J, R, C, N, E = 512, 1024, 1024, 256, 512, 512, 256, 1024
+FLOPS = 2 * J * (K * R + K * R + R * N + K * N)
+
+F32 = mybir.dt.float32
+BF16 = mybir.dt.bfloat16
+I32 = mybir.dt.int32
+U32 = mybir.dt.uint32
+U16 = mybir.dt.uint16
+U8 = mybir.dt.uint8
+E4M3 = mybir.dt.float8_e4m3fn_x4
+E5M2 = mybir.dt.float8_e5m2_x4
+E2M1 = mybir.dt.float4_e2m1fn_x4
+ALU = mybir.AluOpType
+ACT = mybir.ActivationFunctionType
+
+P = 128
+PACK = 4
+HALF = J // 2
+
+
+def load_words(engine, tile, words):
+    engine.dma_start(out=tile[:].bitcast(I32), in_=words[0].rearrange("p n t -> p (n t)").bitcast(I32))
+
+
+def load_scales(engine, tile, col0, scales):
+    width = scales.shape[2]
+    rows = scales[0].bitcast(I32)
+    for q in range(4):
+        engine.dma_start(
+            out=tile[32 * q : 32 * q + 4, col0 : col0 + width].bitcast(I32), in_=rows[4 * q : 4 * q + 4, :]
+        )
+
+
+def tile_list_ownboard_bank_further_tabled_kernel(
+    tc, xt_words, xt_scales, w_words, w_scales, xo_words, xo_scales, w0_words, w0_scales,
+    wb_words, wb_scales, ws_words, ws_scales, tz, offs, offs2, offs3, offs4, offs5, offs6, out,
+):
+    nc = tc.nc
+    with ExitStack() as ctx:
+        keep = ctx.enter_context(tc.tile_pool(name="keep", bufs=1))
+        psum = ctx.enter_context(tc.psum_pool(name="psum", bufs=1))
+
+        def sbuf(shape, dtype, name, tag=None):
+            return keep.tile(shape, dtype, name=name, tag=tag or name, align_bytes=64)
+
+        lists = [sbuf([P, J // 16], U16, "list%d" % i) for i in range(6)]
+        l_xt, l_xo, l_put, l_get, l_short, l_tz = lists
+
+        xt_w = sbuf([P, T], U16, "xt_w")
+        xt_s = sbuf([P, T], U8, "xt_s")
+        xo_w = sbuf([P, Z], U32, "xo_w")
+        xo_s = sbuf([P, Z], U8, "xo_s")
+        w_raw = sbuf([P, R], U32, "w_raw")
+        w0_raw = sbuf([P, R], U32, "w0_raw")
+        s1_raw = sbuf([P, 2 * R], U8, "s1_raw")
+        wb_w = sbuf([P, N], U32, "wb_w")
+        ws_w = sbuf([P, N], U32, "ws_w")
+        s2 = sbuf([P, 2 * N], U8, "s2")
+        tz_sb = [sbuf([P, E], F32, "tz%d" % u) for u in range(2)]
+        boards = [sbuf([P, C], F32, "board%d" % t) for t in range(PACK)]
+
+        for plane in (xt_s, s1_raw, xo_s, s2):
+            nc.vector.memset(plane[:].bitcast(I32), 0)
+        for board in boards:
+            nc.vector.memset(board[:], 0.0)
+
+        nc.sync.dma_start(l_xt[:], offs)
+        nc.sync.dma_start(out=xt_w[:].bitcast(I32), in_=xt_words[0].bitcast(I32))
+        load_scales(nc.sync, xt_s, 0, xt_scales)
+        load_words(nc.sync, w_raw, w_words)
+        load_scales(nc.sync, s1_raw, 0, w_scales)
+        nc.sync.dma_start(l_xo[:], offs2)
+        load_words(nc.sync, xo_w, xo_words)
+        load_scales(nc.sync, xo_s, 0, xo_scales)
+        load_words(nc.sync, w0_raw, w0_words)
+        load_scales(nc.sync, s1_raw, R, w0_scales)
+        nc.sync.dma_start(l_short[:], offs5)
+        nc.sync.dma_start(l_put[:], offs3)
+        nc.sync.dma_start(l_get[:], offs4)
+        load_words(nc.sync, ws_w, ws_words)
+        load_scales(nc.sync, s2, N, ws_scales)
+        load_words(nc.sync, wb_w, wb_words)
+        load_scales(nc.sync, s2, 0, wb_scales)
+        nc.sync.dma_start(l_tz[:], offs6)
+        for u in range(2):
+            nc.sync.dma_start(out=tz_sb[u][:], in_=tz[u * P : (u + 1) * P, :])
+
+        def gather(name, window, offsets, dtype):
+            got = sbuf([P, J], dtype, name)
+            nc.vector.tensor_copy(got[:], window[:].indirect(offsets[:]))
+            return got
+
+        w_w = sbuf([P, R], U32, "w_w")
+        w0_w = sbuf([P, R], U32, "w0_w")
+        for dealt, raw in ((w_w, w_raw), (w0_w, w0_raw)):
+            nc.scalar.copy(
+                out=dealt[:].rearrange("p (t b i) -> p b t i", t=PACK, i=4),
+                in_=raw[:].rearrange("p (b i t) -> p b t i", t=PACK, i=4),
+            )
+        s1 = sbuf([P, 2 * R], U8, "s1")
+
+        def deal_scales(m):
+            cols = slice(m * R, (m + 1) * R)
+            nc.vector.tensor_copy(
+                out=s1[:, cols].rearrange("p (t b i) -> p b t i", t=PACK, i=16),
+                in_=s1_raw[:, cols].rearrange("p (b i t) -> p b t i", t=PACK, i=16),
+            )
+
+        g_xt_w = gather("g_xt_w", xt_w, l_xt, U16)
+        g_xt_s = gather("g_xt_s", xt_s, l_xt, U8)
+        deal_scales(0)
+        g_xo_w = gather("g_xo_w", xo_w, l_xo, U32)
+        g_xo_s = gather("g_xo_s", xo_s, l_xo, U8)
+        deal_scales(1)
+
+        a_ps = [psum.tile([P, J], F32, name="a_ps%d" % t) for t in range(PACK)]
+        for t in range(PACK):
+            cols = slice(t * P, (t + 1) * P)
+            nc.tensor.matmul_mx(
+                out=a_ps[t][:], lhsT=w_w[:, cols].bitcast(E5M2), lhsT_scale=s1[:, cols],
+                rhs=g_xt_w[:].bitcast(E2M1), rhs_scale=g_xt_s[:], start=True, stop=False,
+            )
+        for t in range(PACK):
+            cols = slice(t * P, (t + 1) * P)
+            cols0 = slice(R + t * P, R + (t + 1) * P)
+            nc.tensor.matmul_mx(
+                out=a_ps[t][:], lhsT=w0_w[:, cols].bitcast(E4M3), lhsT_scale=s1[:, cols0],
+                rhs=g_xo_w[:].bitcast(E5M2), rhs_scale=g_xo_s[:], start=False, stop=True,
+            )
+
+        g5_w = gather("g5_w", xt_w, l_short, U16)
+        g5_s = gather("g5_s", xt_s, l_short, U8)
+
+        a = [sbuf([P, J], F32, "a%d" % t) for t in range(PACK)]
+        for t in range(PACK):
+            nc.scalar.copy(a[t][:], a_ps[t][:])
+        for t in (0, 1):
+            nc.vector.tensor_copy(boards[t][:].indirect(l_put[:]), a[t][:])
+        for t in (2, 3):
+            nc.scalar.activation(boards[t][:].indirect(l_put[:]), a[t][:], ACT.Copy)
+
+        diff = sbuf([P, PACK, J], F32, "diff")
+        for t in (0, 1):
+            nc.vector.tensor_tensor(diff[:, t, :], boards[t][:].indirect(l_get[:]), a[t][:], ALU.subtract)
+        for t in (2, 3):
+            got = sbuf([P, J], F32, "got%d" % t, tag="picked%d" % (t - 2))
+            nc.scalar.activation(got[:], boards[t][:].indirect(l_get[:]), ACT.Copy)
+            nc.vector.tensor_tensor(diff[:, t, :], got[:], a[t][:], ALU.subtract)
+
+        hid = sbuf([P, J * PACK], BF16, "hid")
+        hid_v = hid[:].rearrange("p (c i t) -> p c t i", t=PACK, i=4)
+        diff_v = diff[:].rearrange("p t (c i) -> p c t i", i=4)
+        cut = HALF // 4
+        nc.scalar.activation(hid_v[:, :cut], diff_v[:, :cut], ACT.Abs)
+        hid_j = hid[:].rearrange("p (j t) -> p j t", t=PACK)
+        diff_j = diff[:].rearrange("p t j -> p j t")
+        nc.vector.scalar_tensor_tensor(
+            hid_j[:, HALF:, :], diff_j[:, HALF:, :], -1.0, diff_j[:, HALF:, :], ALU.mult, ALU.max
+        )
+        hid_w = sbuf([P, J], U32, "hid_w")
+        hid_s = sbuf([P, J], U8, "hid_s")
+        nc.vector.quantize_mx(out=hid_w[:].bitcast(E5M2), scales=hid_s[:], in_=hid[:])
+
+        tz_got = [sbuf([P, J], F32, "tz_got%d" % u, tag="picked%d" % u) for u in range(2)]
+        for u in range(2):
+            nc.scalar.activation(tz_got[u][:], tz_sb[u][:].indirect(l_tz[:]), ACT.Copy)
+
+        p_ps = [psum.tile([P, J], F32, name="p_ps%d" % u) for u in range(2)]
+        for u in range(2):
+            cols = slice(u * P, (u + 1) * P)
+            cols_s = slice(N + u * P, N + (u + 1) * P)
+            nc.tensor.matmul_mx(
+                out=p_ps[u][:], lhsT=ws_w[:, cols].bitcast(E4M3), lhsT_scale=s2[:, cols_s],
+                rhs=g5_w[:].bitcast(E2M1), rhs_scale=g5_s[:], start=True, stop=False,
+            )
+        for u in range(2):
+            cols = slice(u * P, (u + 1) * P)
+            nc.tensor.matmul_mx(
+                out=p_ps[u][:], lhsT=wb_w[:, cols].bitcast(E4M3), lhsT_scale=s2[:, cols],
+                rhs=hid_w[:].bitcast(E5M2), rhs_scale=hid_s[:], start=False, stop=True,
+            )
+            res = sbuf([P, J], F32, "res%d" % u)
+            nc.vector.tensor_tensor(res[:], p_ps[u][:], tz_got[u][:], ALU.add)
+            nc.sync.dma_start(out=out[u * P : (u + 1) * P, :], in_=res[:])

@@ -23,15 +23,18 @@ HALF = J // 2
 
 
 def load_words(engine, tile, words):
-    engine.dma_start(out=tile[:].bitcast(I32), in_=words[0].rearrange("p n t -> p (n t)").bitcast(I32))
+    engine.dma_start(out=tile.bitcast(I32), in_=words[0].rearrange("p n t -> p (n t)").bitcast(I32))
 
 
-def load_scales(engine, tile, col0, scales):
+def load_scale_rows(engine, tile, col0, scales):
     width = scales.shape[2]
-    rows = scales[0].bitcast(I32)
-    for q in range(4):
+    engine.dma_start(out=tile[0:16, col0 : col0 + width].bitcast(I32), in_=scales[0].bitcast(I32))
+
+
+def spread_scale_rows(engine, tile):
+    for q in range(1, 4):
         engine.dma_start(
-            out=tile[32 * q : 32 * q + 4, col0 : col0 + width].bitcast(I32), in_=rows[4 * q : 4 * q + 4, :]
+            out=tile[32 * q : 32 * q + 4, :].bitcast(I32), in_=tile[4 * q : 4 * q + 4, :].bitcast(I32)
         )
 
 
@@ -56,43 +59,49 @@ def tile_list_ownboard_bank_further_tabled_kernel(
         xo_s = sbuf([P, Z], U8, "xo_s")
         w_raw = sbuf([P, R], U32, "w_raw")
         w0_raw = sbuf([P, R], U32, "w0_raw")
-        s1_raw = sbuf([P, 2 * R], U8, "s1_raw")
-        wb_w = sbuf([P, N], U32, "wb_w")
-        ws_w = sbuf([P, N], U32, "ws_w")
-        s2 = sbuf([P, 2 * N], U8, "s2")
-        tz_sb = [sbuf([P, E], F32, "tz%d" % u) for u in range(2)]
+        ws_raw = [sbuf([P, R], U8, "s_raw%d" % m) for m in range(2)]
         boards = [sbuf([P, C], F32, "board%d" % t) for t in range(PACK)]
 
-        for plane in (xt_s, s1_raw, xo_s, s2):
-            nc.vector.memset(plane[:].bitcast(I32), 0)
+        for plane in (xt_s[:], xo_s[:]):
+            nc.gpsimd.memset(plane.bitcast(I32), 0)
+        for plane in (ws_raw[0][:], ws_raw[1][:]):
+            nc.vector.memset(plane.bitcast(I32), 0)
         for board in boards:
             nc.vector.memset(board[:], 0.0)
 
         nc.sync.dma_start(l_xt[:], offs)
-        nc.sync.dma_start(out=xt_w[:].bitcast(I32), in_=xt_words[0].bitcast(I32))
-        load_scales(nc.sync, xt_s, 0, xt_scales)
-        load_words(nc.sync, w_raw, w_words)
-        load_scales(nc.sync, s1_raw, 0, w_scales)
+        load_scale_rows(nc.sync, xt_s, 0, xt_scales)
+        load_scale_rows(nc.sync, ws_raw[0], 0, w_scales)
         nc.sync.dma_start(l_xo[:], offs2)
-        load_words(nc.sync, xo_w, xo_words)
-        load_scales(nc.sync, xo_s, 0, xo_scales)
-        load_words(nc.sync, w0_raw, w0_words)
-        load_scales(nc.sync, s1_raw, R, w0_scales)
+        load_scale_rows(nc.sync, xo_s, 0, xo_scales)
+        load_scale_rows(nc.sync, ws_raw[1], 0, w0_scales)
+        nc.sync.dma_start(out=xt_w[:].bitcast(I32), in_=xt_words[0].bitcast(I32))
+        load_words(nc.sync, w_raw[:], w_words)
         nc.sync.dma_start(l_short[:], offs5)
         nc.sync.dma_start(l_put[:], offs3)
         nc.sync.dma_start(l_get[:], offs4)
-        load_words(nc.sync, ws_w, ws_words)
-        load_scales(nc.sync, s2, N, ws_scales)
-        load_words(nc.sync, wb_w, wb_words)
-        load_scales(nc.sync, s2, 0, wb_scales)
         nc.sync.dma_start(l_tz[:], offs6)
-        for u in range(2):
-            nc.sync.dma_start(out=tz_sb[u][:], in_=tz[u * P : (u + 1) * P, :])
+        load_words(nc.sync, xo_w[:], xo_words)
+        load_words(nc.sync, w0_raw[:], w0_words)
 
         def gather(name, window, offsets, dtype):
             got = sbuf([P, J], dtype, name)
             nc.vector.tensor_copy(got[:], window[:].indirect(offsets[:]))
             return got
+
+        def first_stage_scales(name, raw, window, offsets):
+            plane = sbuf([P, R + J], U8, name)
+            got = gather(name + "_got", window, offsets, U8)
+            nc.vector.tensor_copy(
+                out=plane[:, :R].rearrange("p (t b i) -> p b t i", t=PACK, i=16),
+                in_=raw[:].rearrange("p (b i t) -> p b t i", t=PACK, i=16),
+            )
+            nc.vector.tensor_copy(plane[:, R:].bitcast(I32), got[:].bitcast(I32))
+            spread_scale_rows(nc.sync, plane)
+            return plane
+
+        s_a = first_stage_scales("s_a", ws_raw[0], xt_s, l_xt)
+        s_b = first_stage_scales("s_b", ws_raw[1], xo_s, l_xo)
 
         w_w = sbuf([P, R], U32, "w_w")
         w0_w = sbuf([P, R], U32, "w0_w")
@@ -101,39 +110,41 @@ def tile_list_ownboard_bank_further_tabled_kernel(
                 out=dealt[:].rearrange("p (t b i) -> p b t i", t=PACK, i=4),
                 in_=raw[:].rearrange("p (b i t) -> p b t i", t=PACK, i=4),
             )
-        s1 = sbuf([P, 2 * R], U8, "s1")
-
-        def deal_scales(m):
-            cols = slice(m * R, (m + 1) * R)
-            nc.vector.tensor_copy(
-                out=s1[:, cols].rearrange("p (t b i) -> p b t i", t=PACK, i=16),
-                in_=s1_raw[:, cols].rearrange("p (b i t) -> p b t i", t=PACK, i=16),
-            )
 
         g_xt_w = gather("g_xt_w", xt_w, l_xt, U16)
-        g_xt_s = gather("g_xt_s", xt_s, l_xt, U8)
-        deal_scales(0)
         g_xo_w = gather("g_xo_w", xo_w, l_xo, U32)
-        g_xo_s = gather("g_xo_s", xo_s, l_xo, U8)
-        deal_scales(1)
+
+        s2 = sbuf([P, 2 * N + J], U8, "s2", tag="s_b_got")
+        nc.vector.memset(s2[:, : 2 * N].bitcast(I32), 0)
+        load_scale_rows(nc.sync, s2, 0, wb_scales)
+        load_scale_rows(nc.sync, s2, N, ws_scales)
+
+        g5_w = gather("g5_w", xt_w, l_short, U16)
+        g5_s = gather("g5_s", xt_s, l_short, U8)
+        s_short = s2[:, 2 * N :]
+        nc.vector.tensor_copy(s_short.bitcast(I32), g5_s[:].bitcast(I32))
+        spread_scale_rows(nc.sync, s2)
+        w2 = sbuf([P, 2 * N], U32, "w2", tag="xt_s")
+        wb_w, ws_w = w2[:, :N], w2[:, N:]
+        tz_sb = [sbuf([P, E], F32, "tz%d" % u, tag=("xo_w", "xt_w")[u]) for u in range(2)]
+        load_words(nc.sync, ws_w, ws_words)
+        load_words(nc.sync, wb_w, wb_words)
+        for u in range(2):
+            nc.sync.dma_start(out=tz_sb[u][:], in_=tz[u * P : (u + 1) * P, :])
 
         a_ps = [psum.tile([P, J], F32, name="a_ps%d" % t) for t in range(PACK)]
         for t in range(PACK):
             cols = slice(t * P, (t + 1) * P)
             nc.tensor.matmul_mx(
-                out=a_ps[t][:], lhsT=w_w[:, cols].bitcast(E5M2), lhsT_scale=s1[:, cols],
-                rhs=g_xt_w[:].bitcast(E2M1), rhs_scale=g_xt_s[:], start=True, stop=False,
+                out=a_ps[t][:], lhsT=w_w[:, cols].bitcast(E5M2), lhsT_scale=s_a[:, cols],
+                rhs=g_xt_w[:].bitcast(E2M1), rhs_scale=s_a[:, R:], start=True, stop=False,
             )
         for t in range(PACK):
             cols = slice(t * P, (t + 1) * P)
-            cols0 = slice(R + t * P, R + (t + 1) * P)
             nc.tensor.matmul_mx(
-                out=a_ps[t][:], lhsT=w0_w[:, cols].bitcast(E4M3), lhsT_scale=s1[:, cols0],
-                rhs=g_xo_w[:].bitcast(E5M2), rhs_scale=g_xo_s[:], start=False, stop=True,
+                out=a_ps[t][:], lhsT=w0_w[:, cols].bitcast(E4M3), lhsT_scale=s_b[:, cols],
+                rhs=g_xo_w[:].bitcast(E5M2), rhs_scale=s_b[:, R:], start=False, stop=True,
             )
-
-        g5_w = gather("g5_w", xt_w, l_short, U16)
-        g5_s = gather("g5_s", xt_s, l_short, U8)
 
         a = [sbuf([P, J], F32, "a%d" % t) for t in range(PACK)]
         for t in range(PACK):
@@ -175,7 +186,7 @@ def tile_list_ownboard_bank_further_tabled_kernel(
             cols_s = slice(N + u * P, N + (u + 1) * P)
             nc.tensor.matmul_mx(
                 out=p_ps[u][:], lhsT=ws_w[:, cols].bitcast(E4M3), lhsT_scale=s2[:, cols_s],
-                rhs=g5_w[:].bitcast(E2M1), rhs_scale=g5_s[:], start=True, stop=False,
+                rhs=g5_w[:].bitcast(E2M1), rhs_scale=s_short, start=True, stop=False,
             )
         for u in range(2):
             cols = slice(u * P, (u + 1) * P)

from contextlib import ExitStack

import concourse.mybir as mybir

K, T, Z, J, R, C, N, E = 512, 1024, 1024, 256, 512, 512, 256, 1024
FLOPS = 2 * J * (K * R + K * R + R * N + K * N)

F32 = mybir.dt.float32
BF16 = mybir.dt.bfloat16
I32 = mybir.dt.int32
U32 = mybir.dt.uint32
U16 = mybir.dt.uint16
U8 = mybir.dt.uint8
E4M3 = mybir.dt.float8_e4m3fn_x4
E5M2 = mybir.dt.float8_e5m2_x4
E2M1 = mybir.dt.float4_e2m1fn_x4
ALU = mybir.AluOpType
ACT = mybir.ActivationFunctionType

P = 128
PACK = 4
HALF = J // 2


def load_words(engine, tile, words):
    engine.dma_start(out=tile.bitcast(I32), in_=words[0].rearrange("p n t -> p (n t)").bitcast(I32))


def load_scale_rows(engine, tile, col0, scales):
    width = scales.shape[2]
    engine.dma_start(out=tile[0:16, col0 : col0 + width].bitcast(I32), in_=scales[0].bitcast(I32))


def spread_scale_rows(engine, tile):
    for q in range(1, 4):
        engine.dma_start(
            out=tile[32 * q : 32 * q + 4, :].bitcast(I32), in_=tile[4 * q : 4 * q + 4, :].bitcast(I32)
        )


def tile_list_ownboard_bank_further_tabled_kernel(
    tc, xt_words, xt_scales, w_words, w_scales, xo_words, xo_scales, w0_words, w0_scales,
    wb_words, wb_scales, ws_words, ws_scales, tz, offs, offs2, offs3, offs4, offs5, offs6, out,
):
    nc = tc.nc
    with ExitStack() as ctx:
        keep = ctx.enter_context(tc.tile_pool(name="keep", bufs=1))
        psum = ctx.enter_context(tc.psum_pool(name="psum", bufs=1))

        def sbuf(shape, dtype, name, tag=None):
            return keep.tile(shape, dtype, name=name, tag=tag or name, align_bytes=64)

        lists = [sbuf([P, J // 16], U16, "list%d" % i) for i in range(6)]
        l_xt, l_xo, l_put, l_get, l_short, l_tz = lists

        xt_w = sbuf([P, T], U16, "xt_w")
        xt_s = sbuf([P, T], U8, "xt_s")
        xo_w = sbuf([P, Z], U32, "xo_w")
        xo_s = sbuf([P, Z], U8, "xo_s")
        w_raw = sbuf([P, R], U32, "w_raw")
        w0_raw = sbuf([P, R], U32, "w0_raw")
        ws_raw = [sbuf([P, R], U8, "s_raw%d" % m) for m in range(2)]
        boards = [sbuf([P, C], F32, "board%d" % t) for t in range(PACK)]

        for plane in (xt_s[:], xo_s[:]):
            nc.gpsimd.memset(plane.bitcast(I32), 0)
        for plane in (ws_raw[0][:], ws_raw[1][:]):
            nc.vector.memset(plane.bitcast(I32), 0)
        for board in boards:
            nc.vector.memset(board[:], 0.0)

        nc.sync.dma_start(l_xt[:], offs)
        load_scale_rows(nc.sync, xt_s, 0, xt_scales)
        load_scale_rows(nc.sync, ws_raw[0], 0, w_scales)
        nc.sync.dma_start(l_xo[:], offs2)
        load_scale_rows(nc.sync, xo_s, 0, xo_scales)
        load_scale_rows(nc.sync, ws_raw[1], 0, w0_scales)
        nc.sync.dma_start(out=xt_w[:].bitcast(I32), in_=xt_words[0].bitcast(I32))
        load_words(nc.sync, w_raw[:], w_words)
        nc.sync.dma_start(l_short[:], offs5)
        nc.sync.dma_start(l_put[:], offs3)
        nc.sync.dma_start(l_get[:], offs4)
        nc.sync.dma_start(l_tz[:], offs6)
        load_words(nc.sync, xo_w[:], xo_words)
        load_words(nc.sync, w0_raw[:], w0_words)

        def gather(name, window, offsets, dtype):
            got = sbuf([P, J], dtype, name)
            nc.vector.tensor_copy(got[:], window[:].indirect(offsets[:]))
            return got

        def first_stage_scales(name, raw, window, offsets):
            plane = sbuf([P, R + J], U8, name)
            got = gather(name + "_got", window, offsets, U8)
            nc.vector.tensor_copy(
                out=plane[:, :R].rearrange("p (t b i) -> p b t i", t=PACK, i=16),
                in_=raw[:].rearrange("p (b i t) -> p b t i", t=PACK, i=16),
            )
            nc.vector.tensor_copy(plane[:, R:].bitcast(I32), got[:].bitcast(I32))
            spread_scale_rows(nc.sync, plane)
            return plane

        s_a = first_stage_scales("s_a", ws_raw[0], xt_s, l_xt)
        s_b = first_stage_scales("s_b", ws_raw[1], xo_s, l_xo)

        w_w = sbuf([P, R], U32, "w_w")
        w0_w = sbuf([P, R], U32, "w0_w")
        for dealt, raw in ((w_w, w_raw), (w0_w, w0_raw)):
            nc.scalar.copy(
                out=dealt[:].rearrange("p (t b i) -> p b t i", t=PACK, i=4),
                in_=raw[:].rearrange("p (b i t) -> p b t i", t=PACK, i=4),
            )

        g_xt_w = gather("g_xt_w", xt_w, l_xt, U16)
        g_xo_w = gather("g_xo_w", xo_w, l_xo, U32)

        s2 = sbuf([P, 2 * N + J], U8, "s2", tag="s_b_got")
        nc.vector.memset(s2[:, : 2 * N].bitcast(I32), 0)
        load_scale_rows(nc.sync, s2, 0, wb_scales)
        load_scale_rows(nc.sync, s2, N, ws_scales)

        g5_w = gather("g5_w", xt_w, l_short, U16)
        g5_s = gather("g5_s", xt_s, l_short, U8)
        s_short = s2[:, 2 * N :]
        nc.vector.tensor_copy(s_short.bitcast(I32), g5_s[:].bitcast(I32))
        spread_scale_rows(nc.sync, s2)
        w2 = sbuf([P, 2 * N], U32, "w2", tag="xt_s")
        wb_w, ws_w = w2[:, :N], w2[:, N:]
        tz_sb = [sbuf([P, E], F32, "tz%d" % u, tag=("xo_w", "xt_w")[u]) for u in range(2)]
        load_words(nc.sync, ws_w, ws_words)
        load_words(nc.sync, wb_w, wb_words)
        for u in range(2):
            nc.sync.dma_start(out=tz_sb[u][:], in_=tz[u * P : (u + 1) * P, :])

        a_ps = [psum.tile([P, J], F32, name="a_ps%d" % t) for t in range(PACK)]
        for t in range(PACK):
            cols = slice(t * P, (t + 1) * P)
            nc.tensor.matmul_mx(
                out=a_ps[t][:], lhsT=w_w[:, cols].bitcast(E5M2), lhsT_scale=s_a[:, cols],
                rhs=g_xt_w[:].bitcast(E2M1), rhs_scale=s_a[:, R:], start=True, stop=False,
            )
        for t in range(PACK):
            cols = slice(t * P, (t + 1) * P)
            nc.tensor.matmul_mx(
                out=a_ps[t][:], lhsT=w0_w[:, cols].bitcast(E4M3), lhsT_scale=s_b[:, cols],
                rhs=g_xo_w[:].bitcast(E5M2), rhs_scale=s_b[:, R:], start=False, stop=True,
            )

        a = [sbuf([P, J], F32, "a%d" % t) for t in range(PACK)]
        for t in range(PACK):
            nc.scalar.copy(a[t][:], a_ps[t][:])
        for t in (0, 1):
            nc.vector.tensor_copy(boards[t][:].indirect(l_put[:]), a[t][:])
        for t in (2, 3):
            nc.scalar.activation(boards[t][:].indirect(l_put[:]), a[t][:], ACT.Copy)

        diff = sbuf([P, PACK, J], F32, "diff")
        for t in (0, 1):
            nc.vector.tensor_tensor(diff[:, t, :], boards[t][:].indirect(l_get[:]), a[t][:], ALU.subtract)
        for t in (2, 3):
            got = sbuf([P, J], F32, "got%d" % t, tag="picked%d" % (t - 2))
            nc.scalar.activation(got[:], boards[t][:].indirect(l_get[:]), ACT.Copy)
            nc.vector.tensor_tensor(diff[:, t, :], got[:], a[t][:], ALU.subtract)

        hid = sbuf([P, J * PACK], BF16, "hid")
        hid_v = hid[:].rearrange("p (c i t) -> p c t i", t=PACK, i=4)
        diff_v = diff[:].rearrange("p t (c i) -> p c t i", i=4)
        cut = HALF // 4
        nc.scalar.activation(hid_v[:, :cut], diff_v[:, :cut], ACT.Abs)
        hid_j = hid[:].rearrange("p (j t) -> p j t", t=PACK)
        diff_j = diff[:].rearrange("p t j -> p j t")
        nc.vector.scalar_tensor_tensor(
            hid_j[:, HALF:, :], diff_j[:, HALF:, :], -1.0, diff_j[:, HALF:, :], ALU.mult, ALU.max
        )
        hid_w = sbuf([P, J], U32, "hid_w")
        hid_s = sbuf([P, J], U8, "hid_s")
        nc.vector.quantize_mx(out=hid_w[:].bitcast(E5M2), scales=hid_s[:], in_=hid[:])

        tz_got = [sbuf([P, J], F32, "tz_got%d" % u, tag="picked%d" % u) for u in range(2)]
        for u in range(2):
            nc.scalar.activation(tz_got[u][:], tz_sb[u][:].indirect(l_tz[:]), ACT.Copy)

        p_ps = [psum.tile([P, J], F32, name="p_ps%d" % u) for u in range(2)]
        for u in range(2):
            cols = slice(u * P, (u + 1) * P)
            cols_s = slice(N + u * P, N + (u + 1) * P)
            nc.tensor.matmul_mx(
                out=p_ps[u][:], lhsT=ws_w[:, cols].bitcast(E4M3), lhsT_scale=s2[:, cols_s],
                rhs=g5_w[:].bitcast(E2M1), rhs_scale=s_short, start=True, stop=False,
            )
        for u in range(2):
            cols = slice(u * P, (u + 1) * P)
            nc.tensor.matmul_mx(
                out=p_ps[u][:], lhsT=wb_w[:, cols].bitcast(E4M3), lhsT_scale=s2[:, cols],
                rhs=hid_w[:].bitcast(E5M2), rhs_scale=hid_s[:], start=False, stop=True,
            )
            res = sbuf([P, J], F32, "res%d" % u)
            nc.vector.tensor_tensor(res[:], p_ps[u][:], tz_got[u][:], ALU.add)
            nc.sync.dma_start(out=out[u * P : (u + 1) * P, :], in_=res[:])
